import numpy as np
import ml_dtypes


def mxq(x, axis, fmt="e4m3"):
    dtype, down = {"e4m3": (ml_dtypes.float8_e4m3fn, 7), "e5m2": (ml_dtypes.float8_e5m2, 14)}[fmt]
    v = np.moveaxis(np.asarray(x, np.float32).astype(ml_dtypes.bfloat16).astype(np.float64), axis, -1)
    blocks = v.reshape(v.shape[:-1] + (-1, 32))
    amax = np.abs(blocks).max(-1, keepdims=True)
    byte = np.maximum(np.where(amax > 0, np.frexp(amax)[1] - 1 + 127, 0) - down, 1)
    scale = np.exp2(byte - 127.0)
    codes = (blocks / scale).astype(np.float32).astype(dtype).astype(np.float64)
    return np.moveaxis((codes * scale).reshape(v.shape), -1, axis)


WIDE = False


def mx_kscale(k):
    if not WIDE:
        return np.ones(k)
    levels = np.array([10, -10, 5, -5, 0])
    if k % 512:
        return np.exp2(np.random.permutation(np.resize(levels, k // 32))).repeat(32)
    a = np.empty((k // 512, 16))
    for p in range(k // 512):
        a[p, :8] = np.random.permutation(np.resize(levels, 8))
        for g in range(8):
            far = levels[np.abs(levels - a[p, g]) >= 10]
            a[p, g + 8] = far[np.random.randint(len(far))]
    return np.exp2(a.ravel()).repeat(32)


BF16 = ml_dtypes.bfloat16


def bf(x):
    return np.asarray(x, np.float32).astype(BF16)


def f64(x):
    return np.asarray(x).astype(np.float64)


E2M1 = np.array([0.0, 0.5, 1.0, 1.5, 2.0, 3.0, 4.0, 6.0, -0.0, -0.5, -1.0, -1.5, -2.0, -3.0, -4.0, -6.0])


def pack_weight(w, fmt):
    k, n = w.shape
    w = f64(bf(w)).reshape(k // 32, 32, n)
    amax = np.abs(w).max(1)
    if fmt == "e4m3":
        byte = np.frexp(amax)[1] - 1 + 127 - 7
    else:
        mant, ex = np.frexp(amax / 6.0)
        byte = np.where(mant > 0.5, ex, ex - 1) + 127
    byte = np.clip(np.where(amax > 0, byte, 1), 1, 254)
    scaled = (w * np.exp2(127.0 - byte)[:, None, :]).reshape(k, n).astype(np.float32)
    by_word = np.ascontiguousarray(scaled.reshape(k // 512, 128, 4, n).transpose(0, 1, 3, 2))
    if fmt == "e4m3":
        words = by_word.astype(ml_dtypes.float8_e4m3fn).view(np.uint8)
    else:
        c = by_word.astype(ml_dtypes.float4_e2m1fn).view(np.uint8) & 0xF
        words = c[..., 0::2] | (c[..., 1::2] << 4)
    return np.ascontiguousarray(words), np.ascontiguousarray(byte.astype(np.uint8).reshape(k // 512, 16, n))


def unpack_weight(words, scales, fmt):
    g, p, n, _ = words.shape
    if fmt == "e4m3":
        vals = np.ascontiguousarray(words).view(ml_dtypes.float8_e4m3fn).astype(np.float64)
    else:
        nib = np.empty((g, p, n, 4), np.uint8)
        nib[..., 0::2] = words & 0xF
        nib[..., 1::2] = words >> 4
        vals = E2M1[nib]
    vals = vals * np.repeat(np.exp2(scales.astype(np.float64) - 127.0), 8, axis=1)[..., None]
    return vals.transpose(0, 1, 3, 2).reshape(g * 512, n)
def pack4(w):
    words, scales = pack_weight(w, "e2m1")
    return words.reshape(words.shape[0], 128, -1), scales


def unpack4(words, scales):
    return unpack_weight(words.reshape(words.shape[0], 128, -1, 2), scales, "e2m1")


M, F, D, R, S = 2048, 2048, 512, 512, 2048


def setup_inputs():
    f = mx_kscale(F)
    r = mx_kscale(R)
    t = mx_kscale(D)
    severity = np.exp(0.4 * np.random.standard_normal((M, 1)))
    common = np.exp(0.4 * np.random.standard_normal((1, S)))
    x = np.random.standard_normal((M, F)) * severity
    w = 3.0 * np.random.standard_normal((F, D)) / np.sqrt(F * D)
    u = np.random.standard_normal((R, D)) ** 4 / (3.0 * np.sqrt(R))
    v = np.random.standard_normal((R, S)) ** 4 * common / (3.0 * np.sqrt(R * D))
    u_words, u_scales = pack4(u * r[:, None] / t)
    v_words, v_scales = pack4(v / r[:, None])
    return {"x": bf(x * f),
            "w": bf(w / f[:, None] * t),
            "u_words": u_words, "u_scales": u_scales,
            "v_words": v_words, "v_scales": v_scales}


def reference(x, w, u_words, u_scales, v_words, v_scales):
    a = np.maximum(mxq(f64(x), 1, "e4m3") @ mxq(f64(w), 0, "e4m3"), 0.0)
    theta = unpack4(u_words, u_scales).T @ unpack4(v_words, v_scales)
    z = mxq(a, 1, "e4m3") @ mxq(theta, 0, "e4m3")
    return 1.0 - np.exp(-z)

@@ -1,0 +1,346 @@
+from contextlib import ExitStack
+
+import concourse.mybir as mybir
+from concourse.masks import make_identity
+
+M, F, D, R, S = 2048, 2048, 512, 512, 2048
+FLOPS = 2 * M * F * D + 2 * D * R * S + 2 * M * D * S
+
+F32 = mybir.dt.float32
+BF16 = mybir.dt.bfloat16
+I32 = mybir.dt.int32
+U32 = mybir.dt.uint32
+U8 = mybir.dt.uint8
+FP8X4 = mybir.dt.float8_e4m3fn_x4
+FP4X4 = mybir.dt.float4_e2m1fn_x4
+ACT = mybir.ActivationFunctionType
+ALU = mybir.AluOpType
+
+P = 128
+PACK = 4
+K_PASS = P * PACK
+BANK = 512
+TILES = M // P
+PASSES = F // K_PASS
+CHUNKS = S // BANK
+
+GROUP = 1
+LEAD = 2
+FIRST_Z_ROUND = 3
+TAIL_CHUNKS = 6
+HEAD_THETA = 3
+THETA_PER_ROUND = 1
+ACT_XT_UNTIL = 6
+ACT_XT_OF4 = 3
+SORT_FROM = 7
+SORT_TO = 16
+SORT_AHEAD = 0
+SORT_ROUNDS = 1
+DELAY_QX = 3
+DELAY_QA = 3
+DELAY_FIN = 2
+DELAY_TH = 7
+ORDER = "u us w0 v w1 vs x0 w2 w3 x1"
+HEAD = "u w0 w1 w2 w3 t0 x0 t1 x1 t2"
+FINE_FROM = 56
+Z_FIRST = 1
+A_FIRST_ROUNDS = 0
+TH_DVE = []
+TH_BUFS = 4
+
+
+def tile_noisy_or_symptom_prediction_s12_kernel(tc, x, w, u_words, u_scales, v_words, v_scales, out):
+    nc = tc.nc
+    with ExitStack() as ctx:
+        keep = ctx.enter_context(tc.tile_pool(name="keep", bufs=1))
+        stage = ctx.enter_context(tc.tile_pool(name="stage", bufs=3))
+        psum = ctx.enter_context(tc.psum_pool(name="psum", bufs=1))
+        ctx.enter_context(tc.manual_schedule())
+
+        def kept(name, shape, dtype):
+            return keep.tile(shape, dtype, name=name, align_bytes=64)
+
+        def staged(name, shape, dtype, bufs):
+            return stage.tile(shape, dtype, name=name, tag=name, bufs=bufs, align_bytes=64)
+
+        w_raw = [kept("w_raw%d" % g, [P, PACK * D], BF16) for g in range(PASSES)]
+        x_raw = [kept("x_raw%d" % i, [P, F], BF16) for i in range(TILES)]
+        u_raw = kept("u_raw", [P, 2 * D], U8)
+        us_raw = kept("us_raw", [P, D], U8)
+        u_sorted = kept("u_sorted", [P, 2 * D], U8)
+        us_sorted = kept("us_sorted", [P, D], U8)
+        v_sb = kept("v_sb", [P, 2 * S], U8)
+        vs_sb = kept("vs_sb", [P, S], U8)
+        w_codes = [kept("w_codes%d" % g, [P, D], U32) for g in range(PASSES)]
+        w_planes = [kept("w_plane%d" % g, [P, D], U8) for g in range(PASSES)]
+        th_codes = [kept("th_codes%d" % c, [P, BANK], U32) for c in range(CHUNKS)]
+        th_planes = [kept("th_plane%d" % c, [P, BANK], U8) for c in range(CHUNKS)]
+        a_codes = [kept("a_codes%d" % i, [P, P], U32) for i in range(TILES)]
+        a_planes = [kept("a_plane%d" % i, [P, P], U8) for i in range(TILES)]
+        ident = kept("ident", [P, P], F32)
+        warm = kept("warm", [P, 16], F32)
+
+        nc.vector.memset(us_raw[:].bitcast(I32), 0)
+        nc.vector.memset(vs_sb[:].bitcast(I32), 0)
+        make_identity(nc, ident[:])
+
+        def load_w(g):
+            rows = w[g * K_PASS : (g + 1) * K_PASS, :]
+            nc.sync.dma_start(out=w_raw[g][:], in_=rows.rearrange("(p j) c -> p (j c)", j=PACK))
+
+        def load_x(i):
+            nc.sync.dma_start(out=x_raw[i][:], in_=x[i * P : (i + 1) * P, :])
+
+        def load_scales(plane, scales):
+            for q in range(4):
+                nc.scalar.dma_start(
+                    out=plane[32 * q : 32 * q + 4, :].bitcast(I32),
+                    in_=scales[0, 4 * q : 4 * q + 4, :].bitcast(I32),
+                )
+
+        def load_u():
+            nc.sync.dma_start(out=u_raw[:].bitcast(I32), in_=u_words[0].bitcast(I32))
+
+        def load_v():
+            nc.sync.dma_start(out=v_sb[:].bitcast(I32), in_=v_words[0].bitcast(I32))
+
+        order = ORDER
+        for name in order.split():
+            if name == "u":
+                load_u()
+            elif name == "v":
+                load_v()
+            elif name == "us":
+                load_scales(us_raw, u_scales)
+                nc.scalar.activation(out=warm[:, 0:1], in_=ident[:, 0:1], func=ACT.Exp)
+            elif name == "vs":
+                load_scales(vs_sb, v_scales)
+            elif name[0] == "w":
+                load_w(int(name[1]))
+            else:
+                load_x(int(name[1]))
+        for i in range(2, TILES):
+            load_x(i)
+
+        free_banks = list(range(8))
+
+        def take_bank():
+            b = free_banks.pop(0)
+            return b, psum.tile([P, BANK], F32, name="bank%d" % b, tag="bank%d" % b)
+
+        def quantize(codes, plane, grouped):
+            nc.vector.quantize_mx(out=codes.bitcast(FP8X4), scales=plane, in_=grouped)
+
+        def prepare_w(g):
+            grouped = staged("w_grouped", [P, PACK * D], BF16, 2)
+            src = w_raw[g][:].rearrange("p (j Q t i) -> p Q t j i", j=PACK, t=PACK, i=4)
+            dst = grouped[:].rearrange("p (t Q i j) -> p Q t j i", t=PACK, i=4, j=PACK)
+            for h in range(2):
+                nc.vector.tensor_copy(out=dst[:, :, 2 * h : 2 * h + 2], in_=src[:, :, 2 * h : 2 * h + 2])
+            for h in range(2):
+                cols = slice(h * D // 2, (h + 1) * D // 2)
+                quantize(w_codes[g][:, cols], w_planes[g][:, cols], grouped[:, h * 2 * D : (h + 1) * 2 * D])
+
+        def sort_u():
+            nc.vector.tensor_copy(
+                out=u_sorted[:].bitcast(I32).rearrange("p (t Q h) -> p t Q h", t=PACK, h=2),
+                in_=u_raw[:].bitcast(I32).rearrange("p (Q t h) -> p t Q h", t=PACK, h=2),
+            )
+            nc.vector.tensor_copy(
+                out=us_sorted[:].bitcast(I32).rearrange("p (t Q) -> p t Q", t=PACK),
+                in_=us_raw[:].bitcast(I32).rearrange("p (Q t) -> p t Q", t=PACK),
+            )
+
+        pending = []
+
+        def later(steps, work):
+            pending.append([steps, work])
+
+        def step_done():
+            for entry in list(pending):
+                entry[0] = entry[0] - 1
+                if entry[0] <= 0:
+                    pending.remove(entry)
+                    entry[1]()
+
+        x_grouped, x_codes, x_planes, th_rows, a_banks, e_tiles = {}, {}, {}, {}, {}, {}
+
+        x_sorted = {}
+
+        def sort_x(i):
+            if SORT_FROM <= i < SORT_TO:
+                x_sorted[i] = staged("x_sorted", [P, F // 2], F32, 4)
+                nc.vector.tensor_copy(
+                    out=x_sorted[i][:].rearrange("p (g u k) -> p g u k", g=PASSES, u=2),
+                    in_=x_raw[i][:].bitcast(F32).rearrange("p (g k u) -> p g u k", g=PASSES, u=2),
+                )
+
+        def transpose_x(i, half):
+            if half == 0:
+                x_grouped[i] = staged("x_grouped", [P, F], BF16, 4)
+            b, bank = take_bank()
+            for g2 in range(2):
+                g = 2 * half + g2
+                for u in range(2):
+                    slot = 2 * g2 + u
+                    if i in x_sorted:
+                        cols = x_sorted[i][:, 256 * g + P * u : 256 * g + P * (u + 1)]
+                    else:
+                        cols = x_raw[i][:].bitcast(F32)[:, 256 * g + u : 256 * (g + 1) : 2]
+                    nc.tensor.transpose(bank[:, slot * P : (slot + 1) * P], cols, ident[:])
+            src = bank[:].rearrange("p (g u m) -> p g m u", g=2, u=2)
+            dst = x_grouped[i][:].bitcast(F32)[:, half * BANK : (half + 1) * BANK]
+            dst = dst.rearrange("p (g m u) -> p g m u", g=2, u=2)
+            if i < ACT_XT_UNTIL or (2 * i + half) % 4 in [[], [0], [0, 2], [0, 1, 2], [0, 1, 2, 3]][ACT_XT_OF4]:
+                nc.scalar.copy(out=dst, in_=src)
+            else:
+                nc.vector.tensor_copy(out=dst, in_=src)
+            free_banks.append(b)
+            if half == 1:
+                later(DELAY_QX, lambda: quantize_x(i))
+            step_done()
+
+        def quantize_x(i):
+            x_codes[i] = staged("x_codes", [P, PASSES * P], U32, 6)
+            x_planes[i] = staged("x_plane", [P, PASSES * P], U8, 6)
+            quantize(x_codes[i][:], x_planes[i][:], x_grouped[i][:])
+
+        def theta_rows(c, t):
+            if t == 0:
+                th_rows[c] = staged("th_rows", [P, PACK * BANK], BF16, TH_BUFS)
+            b, bank = take_bank()
+            nc.tensor.matmul_mx(
+                out=bank[:],
+                lhsT=u_sorted[:, 2 * P * t : 2 * P * (t + 1)].bitcast(FP4X4),
+                lhsT_scale=us_sorted[:, P * t : P * (t + 1)],
+                rhs=v_sb[:, 2 * BANK * c : 2 * BANK * (c + 1)].bitcast(FP4X4),
+                rhs_scale=vs_sb[:, BANK * c : BANK * (c + 1)],
+                start=True,
+                stop=True,
+            )
+            if PACK * c + t in TH_DVE:
+                nc.vector.tensor_copy(out=th_rows[c][:, BANK * t : BANK * (t + 1)], in_=bank[:])
+            else:
+                nc.scalar.copy(out=th_rows[c][:, BANK * t : BANK * (t + 1)], in_=bank[:])
+            free_banks.append(b)
+            if t == PACK - 1:
+                later(DELAY_TH, lambda: prepare_theta(c))
+            step_done()
+
+        def prepare_theta(c):
+            grouped = staged("th_grouped", [P, PACK * BANK], BF16, 2)
+            src = th_rows[c][:].rearrange("p (t s i) -> p s t i", t=PACK, i=4)
+            dst = grouped[:].rearrange("p (s i t) -> p s t i", t=PACK, i=4)
+            for h in range(2):
+                nc.vector.tensor_copy(out=dst[:, 64 * h : 64 * (h + 1)], in_=src[:, 64 * h : 64 * (h + 1)])
+            for h in range(2):
+                cols = slice(h * BANK // 2, (h + 1) * BANK // 2)
+                quantize(th_codes[c][:, cols], th_planes[c][:, cols], grouped[:, h * 2 * BANK : (h + 1) * 2 * BANK])
+
+        def intensities(i, t):
+            if t == 0:
+                a_banks[i] = take_bank()
+            b, bank = a_banks[i]
+            for g in range(PASSES):
+                nc.tensor.matmul_mx(
+                    out=bank[:, P * t : P * (t + 1)],
+                    lhsT=w_codes[g][:, P * t : P * (t + 1)].bitcast(FP8X4),
+                    lhsT_scale=w_planes[g][:, P * t : P * (t + 1)],
+                    rhs=x_codes[i][:, P * g : P * (g + 1)].bitcast(FP8X4),
+                    rhs_scale=x_planes[i][:, P * g : P * (g + 1)],
+                    start=(g == 0),
+                    stop=(g == PASSES - 1),
+                )
+            if t == PACK - 1:
+                grouped = staged("a_grouped", [P, PACK * P], BF16, 2)
+                nc.vector.tensor_scalar(
+                    out=grouped[:].rearrange("p (m t) -> p m t", t=PACK),
+                    in0=bank[:].rearrange("p (t m) -> p m t", t=PACK),
+                    scalar1=0.0,
+                    scalar2=None,
+                    op0=ALU.max,
+                )
+                free_banks.append(b)
+                later(DELAY_QA, lambda: quantize(a_codes[i][:], a_planes[i][:], grouped[:]))
+            step_done()
+
+        def symptoms(n):
+            i, c = divmod(n, CHUNKS)
+            pair = n // 2
+            if c % 2 == 0:
+                e_tiles[pair] = staged("e", [P, 2 * BANK], F32, 6)
+            b, bank = take_bank()
+            nc.tensor.matmul_mx(
+                out=bank[:],
+                lhsT=a_codes[i][:].bitcast(FP8X4),
+                lhsT_scale=a_planes[i][:],
+                rhs=th_codes[c][:].bitcast(FP8X4),
+                rhs_scale=th_planes[c][:],
+                start=True,
+                stop=True,
+            )
+            cols = slice((c % 2) * BANK, (c % 2 + 1) * BANK)
+            nc.scalar.activation(out=e_tiles[pair][:, cols], in_=bank[:], func=ACT.Exp, scale=-1.0)
+            free_banks.append(b)
+            if n >= FINE_FROM:
+                later(DELAY_FIN, lambda: finish(pair, c % 2, c % 2 + 1))
+            elif c % 2 == 1:
+                later(DELAY_FIN, lambda: finish(pair, 0, 2))
+            step_done()
+
+        def finish(pair, first, last):
+            i, half = divmod(pair, 2)
+            e = e_tiles[pair][:, first * BANK : last * BANK]
+            nc.vector.tensor_scalar(out=e, in0=e, scalar1=-1.0, scalar2=1.0, op0=ALU.mult, op1=ALU.add)
+            nc.sync.dma_start(out=out[i * P : (i + 1) * P, (2 * half + first) * BANK : (2 * half + last) * BANK], in_=e)
+
+
+        for name in HEAD.split():
+            if name[0] == "x":
+                for half in range(2):
+                    transpose_x(int(name[1]), half)
+            elif name[0] == "w":
+                prepare_w(int(name[1]))
+            elif name[0] == "u":
+                sort_u()
+            elif name[0] == "s":
+                sort_x(int(name[1]))
+            else:
+                for t in range(PACK):
+                    theta_rows(int(name[1]), t)
+
+        rounds = TILES // GROUP
+        woven = TILES * CHUNKS - TAIL_CHUNKS
+        theta_left = [(c, t) for c in range(HEAD_THETA, CHUNKS) for t in range(PACK)]
+        done = 0
+        for r in range(rounds):
+            if r + LEAD < rounds:
+                for i in range(GROUP * (r + LEAD), GROUP * (r + LEAD + 1)):
+                    for half in range(2):
+                        transpose_x(i, half)
+            due = max(0, woven * (r + 1 - FIRST_Z_ROUND) // (rounds - FIRST_Z_ROUND))
+            count = due - done
+            slots = GROUP * PACK
+            for k in range(slots):
+                if k % PACK == SORT_AHEAD % PACK:
+                    sort_x(GROUP * (r + LEAD + 1 + SORT_ROUNDS) + k // PACK)
+                if r >= rounds - A_FIRST_ROUNDS:
+                    lo, hi = (0, 0)
+                elif Z_FIRST:
+                    lo, hi = -(-count * k // slots), -(-count * (k + 1) // slots)
+                else:
+                    lo, hi = count * k // slots, count * (k + 1) // slots
+                for n in range(done + lo, done + hi):
+                    symptoms(n)
+                for j in range(THETA_PER_ROUND * PACK * (k + 1) // slots - THETA_PER_ROUND * PACK * k // slots):
+                    if theta_left:
+                        theta_rows(*theta_left.pop(0))
+                intensities(GROUP * r + k // PACK, k % PACK)
+            if r >= rounds - A_FIRST_ROUNDS:
+                for n in range(done, due):
+                    symptoms(n)
+            done = due
+        for n in range(done, TILES * CHUNKS):
+            symptoms(n)
+        while pending:
+            step_done()

@@ -32,7 +32,7 @@ HEAD_THETA = 3
 THETA_PER_ROUND = 1
 ACT_XT_UNTIL = 6
 ACT_XT_OF4 = 3
-SORT_FROM = 7
+SORT_FROM = 5
 SORT_TO = 16
 SORT_AHEAD = 0
 SORT_ROUNDS = 1
@@ -40,10 +40,12 @@ DELAY_QX = 3
 DELAY_QA = 3
 DELAY_FIN = 2
 DELAY_TH = 7
-ORDER = "u us w0 v w1 vs x0 w2 w3 x1"
+ORDER = "u us w0 v vs w1 x0 w2 w3 x1"
 HEAD = "u w0 w1 w2 w3 t0 x0 t1 x1 t2"
 FINE_FROM = 56
 Z_FIRST = 1
+ACT_A_UNTIL = 3
+TH_MANUAL = 0
 A_FIRST_ROUNDS = 0
 TH_DVE = []
 TH_BUFS = 4
@@ -93,7 +95,7 @@ def tile_noisy_or_symptom_prediction_s12_kernel(tc, x, w, u_words, u_scales, v_w
 
         def load_scales(plane, scales):
             for q in range(4):
-                nc.scalar.dma_start(
+                nc.sync.dma_start(
                     out=plane[32 * q : 32 * q + 4, :].bitcast(I32),
                     in_=scales[0, 4 * q : 4 * q + 4, :].bitcast(I32),
                 )
@@ -223,7 +225,7 @@ def tile_noisy_or_symptom_prediction_s12_kernel(tc, x, w, u_words, u_scales, v_w
             else:
                 nc.scalar.copy(out=th_rows[c][:, BANK * t : BANK * (t + 1)], in_=bank[:])
             free_banks.append(b)
-            if t == PACK - 1:
+            if t == PACK - 1 and c >= TH_MANUAL:
                 later(DELAY_TH, lambda: prepare_theta(c))
             step_done()
 
@@ -253,13 +255,12 @@ def tile_noisy_or_symptom_prediction_s12_kernel(tc, x, w, u_words, u_scales, v_w
                 )
             if t == PACK - 1:
                 grouped = staged("a_grouped", [P, PACK * P], BF16, 2)
-                nc.vector.tensor_scalar(
-                    out=grouped[:].rearrange("p (m t) -> p m t", t=PACK),
-                    in0=bank[:].rearrange("p (t m) -> p m t", t=PACK),
-                    scalar1=0.0,
-                    scalar2=None,
-                    op0=ALU.max,
-                )
+                dst = grouped[:].rearrange("p (m t) -> p m t", t=PACK)
+                src = bank[:].rearrange("p (t m) -> p m t", t=PACK)
+                if i < ACT_A_UNTIL:
+                    nc.scalar.activation(out=dst, in_=src, func=ACT.Relu)
+                else:
+                    nc.vector.tensor_scalar(out=dst, in0=src, scalar1=0.0, scalar2=None, op0=ALU.max)
                 free_banks.append(b)
                 later(DELAY_QA, lambda: quantize(a_codes[i][:], a_planes[i][:], grouped[:]))
             step_done()
@@ -303,6 +304,8 @@ def tile_noisy_or_symptom_prediction_s12_kernel(tc, x, w, u_words, u_scales, v_w
                 prepare_w(int(name[1]))
             elif name[0] == "u":
                 sort_u()
+            elif name[0] == "p":
+                prepare_theta(int(name[1]))
             elif name[0] == "s":
                 sort_x(int(name[1]))
             else:

@@ -1,3 +1,4 @@
+import math
 from contextlib import ExitStack
 
 import concourse.mybir as mybir
@@ -17,45 +18,29 @@ ACT = mybir.ActivationFunctionType
 ALU = mybir.AluOpType
 
 P = 128
-PACK = 4
-K_PASS = P * PACK
+SLOTS = 4
+K_PASS = P * SLOTS
 BANK = 512
+BANKS = 8
 TILES = M // P
 PASSES = F // K_PASS
 CHUNKS = S // BANK
+PASS_WORDS = K_PASS // 2
 
-GROUP = 1
 LEAD = 2
 FIRST_Z_ROUND = 3
 TAIL_CHUNKS = 6
-HEAD_THETA = 3
-THETA_PER_ROUND = 1
-ACT_XT_UNTIL = 6
-ACT_XT_OF4 = 3
+PAIRS_FROM = 4
 SORT_FROM = 5
-SORT_TO = 16
-SORT_AHEAD = 0
-SORT_ROUNDS = 1
-DELAY_QX = 3
-DELAY_QA = 3
-DELAY_FIN = 2
-DELAY_TH = 7
-ORDER = "u us w0 v vs w1 x0 w2 w3 x1"
-HEAD = "u w0 w1 w2 w3 t0 x0 t1 x1 t2"
-FINE_FROM = 56
-Z_FIRST = 1
-ACT_A_UNTIL = 3
-TH_MANUAL = 0
-A_FIRST_ROUNDS = 0
-TH_DVE = []
-TH_BUFS = 4
+VECTOR_BANK_EVERY = 4
+DELAY = 3
 
 
 def tile_noisy_or_symptom_prediction_s12_kernel(tc, x, w, u_words, u_scales, v_words, v_scales, out):
     nc = tc.nc
     with ExitStack() as ctx:
         keep = ctx.enter_context(tc.tile_pool(name="keep", bufs=1))
-        stage = ctx.enter_context(tc.tile_pool(name="stage", bufs=3))
+        stage = ctx.enter_context(tc.tile_pool(name="stage", bufs=1))
         psum = ctx.enter_context(tc.psum_pool(name="psum", bufs=1))
         ctx.enter_context(tc.manual_schedule())
 
@@ -65,93 +50,62 @@ def tile_noisy_or_symptom_prediction_s12_kernel(tc, x, w, u_words, u_scales, v_w
         def staged(name, shape, dtype, bufs):
             return stage.tile(shape, dtype, name=name, tag=name, bufs=bufs, align_bytes=64)
 
-        w_raw = [kept("w_raw%d" % g, [P, PACK * D], BF16) for g in range(PASSES)]
+        w_raw = [kept("w_raw%d" % g, [P, SLOTS * D], BF16) for g in range(PASSES)]
         x_raw = [kept("x_raw%d" % i, [P, F], BF16) for i in range(TILES)]
         u_raw = kept("u_raw", [P, 2 * D], U8)
-        us_raw = kept("us_raw", [P, D], U8)
-        u_sorted = kept("u_sorted", [P, 2 * D], U8)
-        us_sorted = kept("us_sorted", [P, D], U8)
-        v_sb = kept("v_sb", [P, 2 * S], U8)
-        vs_sb = kept("vs_sb", [P, S], U8)
+        u_raw_plane = kept("u_raw_plane", [P, D], U8)
+        u_codes = kept("u_codes", [P, 2 * D], U8)
+        u_plane = kept("u_plane", [P, D], U8)
+        v_codes = kept("v_codes", [P, 2 * S], U8)
+        v_plane = kept("v_plane", [P, S], U8)
         w_codes = [kept("w_codes%d" % g, [P, D], U32) for g in range(PASSES)]
         w_planes = [kept("w_plane%d" % g, [P, D], U8) for g in range(PASSES)]
-        th_codes = [kept("th_codes%d" % c, [P, BANK], U32) for c in range(CHUNKS)]
-        th_planes = [kept("th_plane%d" % c, [P, BANK], U8) for c in range(CHUNKS)]
+        theta_codes = [kept("theta_codes%d" % c, [P, BANK], U32) for c in range(CHUNKS)]
+        theta_planes = [kept("theta_plane%d" % c, [P, BANK], U8) for c in range(CHUNKS)]
         a_codes = [kept("a_codes%d" % i, [P, P], U32) for i in range(TILES)]
         a_planes = [kept("a_plane%d" % i, [P, P], U8) for i in range(TILES)]
         ident = kept("ident", [P, P], F32)
         warm = kept("warm", [P, 16], F32)
 
-        nc.vector.memset(us_raw[:].bitcast(I32), 0)
-        nc.vector.memset(vs_sb[:].bitcast(I32), 0)
+        nc.vector.memset(u_raw_plane[:].bitcast(I32), 0)
+        nc.vector.memset(v_plane[:].bitcast(I32), 0)
         make_identity(nc, ident[:])
+        nc.scalar.activation(out=warm[:, 0:1], in_=ident[:, 0:1], func=ACT.Exp)
+
+        def load_bytes(tile, words):
+            nc.sync.dma_start(out=tile[:].bitcast(I32), in_=words[0].bitcast(I32))
+
+        def load_plane(plane, scales):
+            for n in range(4):
+                nc.sync.dma_start(
+                    out=plane[32 * n : 32 * n + 4, :].bitcast(I32),
+                    in_=scales[0, 4 * n : 4 * n + 4, :].bitcast(I32),
+                )
 
         def load_w(g):
             rows = w[g * K_PASS : (g + 1) * K_PASS, :]
-            nc.sync.dma_start(out=w_raw[g][:], in_=rows.rearrange("(p j) c -> p (j c)", j=PACK))
+            nc.sync.dma_start(out=w_raw[g][:], in_=rows.rearrange("(p j) d -> p (j d)", j=SLOTS))
 
         def load_x(i):
             nc.sync.dma_start(out=x_raw[i][:], in_=x[i * P : (i + 1) * P, :])
 
-        def load_scales(plane, scales):
-            for q in range(4):
-                nc.sync.dma_start(
-                    out=plane[32 * q : 32 * q + 4, :].bitcast(I32),
-                    in_=scales[0, 4 * q : 4 * q + 4, :].bitcast(I32),
-                )
-
-        def load_u():
-            nc.sync.dma_start(out=u_raw[:].bitcast(I32), in_=u_words[0].bitcast(I32))
-
-        def load_v():
-            nc.sync.dma_start(out=v_sb[:].bitcast(I32), in_=v_words[0].bitcast(I32))
-
-        order = ORDER
-        for name in order.split():
-            if name == "u":
-                load_u()
-            elif name == "v":
-                load_v()
-            elif name == "us":
-                load_scales(us_raw, u_scales)
-                nc.scalar.activation(out=warm[:, 0:1], in_=ident[:, 0:1], func=ACT.Exp)
-            elif name == "vs":
-                load_scales(vs_sb, v_scales)
-            elif name[0] == "w":
-                load_w(int(name[1]))
-            else:
-                load_x(int(name[1]))
-        for i in range(2, TILES):
+        load_bytes(u_raw, u_words)
+        load_plane(u_raw_plane, u_scales)
+        load_w(0)
+        load_bytes(v_codes, v_words)
+        load_plane(v_plane, v_scales)
+        load_w(1)
+        load_x(0)
+        load_w(2)
+        load_w(3)
+        for i in range(1, TILES):
             load_x(i)
 
-        free_banks = list(range(8))
+        free_banks = list(range(BANKS))
 
         def take_bank():
             b = free_banks.pop(0)
             return b, psum.tile([P, BANK], F32, name="bank%d" % b, tag="bank%d" % b)
-
-        def quantize(codes, plane, grouped):
-            nc.vector.quantize_mx(out=codes.bitcast(FP8X4), scales=plane, in_=grouped)
-
-        def prepare_w(g):
-            grouped = staged("w_grouped", [P, PACK * D], BF16, 2)
-            src = w_raw[g][:].rearrange("p (j Q t i) -> p Q t j i", j=PACK, t=PACK, i=4)
-            dst = grouped[:].rearrange("p (t Q i j) -> p Q t j i", t=PACK, i=4, j=PACK)
-            for h in range(2):
-                nc.vector.tensor_copy(out=dst[:, :, 2 * h : 2 * h + 2], in_=src[:, :, 2 * h : 2 * h + 2])
-            for h in range(2):
-                cols = slice(h * D // 2, (h + 1) * D // 2)
-                quantize(w_codes[g][:, cols], w_planes[g][:, cols], grouped[:, h * 2 * D : (h + 1) * 2 * D])
-
-        def sort_u():
-            nc.vector.tensor_copy(
-                out=u_sorted[:].bitcast(I32).rearrange("p (t Q h) -> p t Q h", t=PACK, h=2),
-                in_=u_raw[:].bitcast(I32).rearrange("p (Q t h) -> p t Q h", t=PACK, h=2),
-            )
-            nc.vector.tensor_copy(
-                out=us_sorted[:].bitcast(I32).rearrange("p (t Q) -> p t Q", t=PACK),
-                in_=us_raw[:].bitcast(I32).rearrange("p (Q t) -> p t Q", t=PACK),
-            )
 
         pending = []
 
@@ -161,85 +115,107 @@ def tile_noisy_or_symptom_prediction_s12_kernel(tc, x, w, u_words, u_scales, v_w
         def step_done():
             for entry in list(pending):
                 entry[0] = entry[0] - 1
-                if entry[0] <= 0:
+                if entry[0] == 0:
                     pending.remove(entry)
                     entry[1]()
 
-        x_grouped, x_codes, x_planes, th_rows, a_banks, e_tiles = {}, {}, {}, {}, {}, {}
+        def quantize(codes, plane, grouped):
+            nc.vector.quantize_mx(out=codes.bitcast(FP8X4), scales=plane, in_=grouped)
 
-        x_sorted = {}
+        def quantize_halves(codes, plane, grouped):
+            half = codes.shape[1] // 2
+            for h in range(2):
+                cols = slice(h * half, (h + 1) * half)
+                quantize(codes[:, cols], plane[:, cols], grouped[:, SLOTS * h * half : SLOTS * (h + 1) * half])
+
+        def sort_u():
+            nc.vector.tensor_copy(
+                out=u_codes[:].bitcast(I32).rearrange("p (t Q h) -> p t Q h", t=SLOTS, h=2),
+                in_=u_raw[:].bitcast(I32).rearrange("p (Q t h) -> p t Q h", t=SLOTS, h=2),
+            )
+            nc.vector.tensor_copy(
+                out=u_plane[:].bitcast(I32).rearrange("p (t Q) -> p t Q", t=SLOTS),
+                in_=u_raw_plane[:].bitcast(I32).rearrange("p (Q t) -> p t Q", t=SLOTS),
+            )
+
+        def prepare_w(g):
+            grouped = staged("w_grouped", [P, SLOTS * D], BF16, 2)
+            src = w_raw[g][:].rearrange("p (j Q t i) -> p Q t j i", j=SLOTS, t=SLOTS, i=4)
+            dst = grouped[:].rearrange("p (t Q i j) -> p Q t j i", t=SLOTS, i=4, j=SLOTS)
+            for h in range(2):
+                nc.vector.tensor_copy(out=dst[:, :, 2 * h : 2 * h + 2], in_=src[:, :, 2 * h : 2 * h + 2])
+            quantize_halves(w_codes[g], w_planes[g], grouped)
+
+        theta_rows, x_sorted, x_grouped, x_codes, x_planes, a_banks, e_tiles = {}, {}, {}, {}, {}, {}, {}
+
+        def theta_slot(c, t):
+            if t == 0:
+                theta_rows[c] = staged("theta_rows", [P, SLOTS * BANK], BF16, CHUNKS)
+            b, bank = take_bank()
+            nc.tensor.matmul_mx(
+                out=bank[:],
+                lhsT=u_codes[:, 2 * P * t : 2 * P * (t + 1)].bitcast(FP4X4),
+                lhsT_scale=u_plane[:, P * t : P * (t + 1)],
+                rhs=v_codes[:, 2 * BANK * c : 2 * BANK * (c + 1)].bitcast(FP4X4),
+                rhs_scale=v_plane[:, BANK * c : BANK * (c + 1)],
+                start=True,
+                stop=True,
+            )
+            nc.scalar.copy(out=theta_rows[c][:, BANK * t : BANK * (t + 1)], in_=bank[:])
+            free_banks.append(b)
+            if t == SLOTS - 1:
+                later(2 * DELAY, lambda: prepare_theta(c))
+            step_done()
+
+        def theta_chunk(c):
+            for t in range(SLOTS):
+                theta_slot(c, t)
+
+        def prepare_theta(c):
+            grouped = staged("theta_grouped", [P, SLOTS * BANK], BF16, 2)
+            src = theta_rows[c][:].rearrange("p (t s i) -> p s t i", t=SLOTS, i=4)
+            dst = grouped[:].rearrange("p (s i t) -> p s t i", t=SLOTS, i=4)
+            half = BANK // 4 // 2
+            for h in range(2):
+                nc.vector.tensor_copy(out=dst[:, half * h : half * (h + 1)], in_=src[:, half * h : half * (h + 1)])
+            quantize_halves(theta_codes[c], theta_planes[c], grouped)
 
         def sort_x(i):
-            if SORT_FROM <= i < SORT_TO:
-                x_sorted[i] = staged("x_sorted", [P, F // 2], F32, 4)
-                nc.vector.tensor_copy(
-                    out=x_sorted[i][:].rearrange("p (g u k) -> p g u k", g=PASSES, u=2),
-                    in_=x_raw[i][:].bitcast(F32).rearrange("p (g k u) -> p g u k", g=PASSES, u=2),
-                )
+            x_sorted[i] = staged("x_sorted", [P, F // 2], F32, 4)
+            nc.vector.tensor_copy(
+                out=x_sorted[i][:].rearrange("p (g u k) -> p g u k", g=PASSES, u=2),
+                in_=x_raw[i][:].bitcast(F32).rearrange("p (g k u) -> p g u k", g=PASSES, u=2),
+            )
 
-        def transpose_x(i, half):
-            if half == 0:
-                x_grouped[i] = staged("x_grouped", [P, F], BF16, 4)
-            b, bank = take_bank()
-            for g2 in range(2):
-                g = 2 * half + g2
-                for u in range(2):
-                    slot = 2 * g2 + u
+        def transpose_x(i, on_scalar_only):
+            x_grouped[i] = staged("x_grouped", [P, F], BF16, 4)
+            for half in range(2):
+                b, bank = take_bank()
+                for n in range(4):
+                    g, u = 2 * half + n // 2, n % 2
                     if i in x_sorted:
-                        cols = x_sorted[i][:, 256 * g + P * u : 256 * g + P * (u + 1)]
+                        words = x_sorted[i][:, PASS_WORDS * g + P * u : PASS_WORDS * g + P * (u + 1)]
                     else:
-                        cols = x_raw[i][:].bitcast(F32)[:, 256 * g + u : 256 * (g + 1) : 2]
-                    nc.tensor.transpose(bank[:, slot * P : (slot + 1) * P], cols, ident[:])
-            src = bank[:].rearrange("p (g u m) -> p g m u", g=2, u=2)
-            dst = x_grouped[i][:].bitcast(F32)[:, half * BANK : (half + 1) * BANK]
-            dst = dst.rearrange("p (g m u) -> p g m u", g=2, u=2)
-            if i < ACT_XT_UNTIL or (2 * i + half) % 4 in [[], [0], [0, 2], [0, 1, 2], [0, 1, 2, 3]][ACT_XT_OF4]:
-                nc.scalar.copy(out=dst, in_=src)
-            else:
-                nc.vector.tensor_copy(out=dst, in_=src)
-            free_banks.append(b)
-            if half == 1:
-                later(DELAY_QX, lambda: quantize_x(i))
-            step_done()
+                        words = x_raw[i][:].bitcast(F32)[:, PASS_WORDS * g + u : PASS_WORDS * (g + 1) : 2]
+                    nc.tensor.transpose(bank[:, n * P : (n + 1) * P], words, ident[:])
+                src = bank[:].rearrange("p (g u m) -> p g m u", g=2, u=2)
+                dst = x_grouped[i][:].bitcast(F32)[:, half * BANK : (half + 1) * BANK]
+                dst = dst.rearrange("p (g m u) -> p g m u", g=2, u=2)
+                if on_scalar_only or (2 * i + half + 1) % VECTOR_BANK_EVERY != 0:
+                    nc.scalar.copy(out=dst, in_=src)
+                else:
+                    nc.vector.tensor_copy(out=dst, in_=src)
+                free_banks.append(b)
+                if half == 1:
+                    later(DELAY, lambda: quantize_x(i))
+                step_done()
 
         def quantize_x(i):
             x_codes[i] = staged("x_codes", [P, PASSES * P], U32, 6)
             x_planes[i] = staged("x_plane", [P, PASSES * P], U8, 6)
             quantize(x_codes[i][:], x_planes[i][:], x_grouped[i][:])
 
-        def theta_rows(c, t):
-            if t == 0:
-                th_rows[c] = staged("th_rows", [P, PACK * BANK], BF16, TH_BUFS)
-            b, bank = take_bank()
-            nc.tensor.matmul_mx(
-                out=bank[:],
-                lhsT=u_sorted[:, 2 * P * t : 2 * P * (t + 1)].bitcast(FP4X4),
-                lhsT_scale=us_sorted[:, P * t : P * (t + 1)],
-                rhs=v_sb[:, 2 * BANK * c : 2 * BANK * (c + 1)].bitcast(FP4X4),
-                rhs_scale=vs_sb[:, BANK * c : BANK * (c + 1)],
-                start=True,
-                stop=True,
-            )
-            if PACK * c + t in TH_DVE:
-                nc.vector.tensor_copy(out=th_rows[c][:, BANK * t : BANK * (t + 1)], in_=bank[:])
-            else:
-                nc.scalar.copy(out=th_rows[c][:, BANK * t : BANK * (t + 1)], in_=bank[:])
-            free_banks.append(b)
-            if t == PACK - 1 and c >= TH_MANUAL:
-                later(DELAY_TH, lambda: prepare_theta(c))
-            step_done()
-
-        def prepare_theta(c):
-            grouped = staged("th_grouped", [P, PACK * BANK], BF16, 2)
-            src = th_rows[c][:].rearrange("p (t s i) -> p s t i", t=PACK, i=4)
-            dst = grouped[:].rearrange("p (s i t) -> p s t i", t=PACK, i=4)
-            for h in range(2):
-                nc.vector.tensor_copy(out=dst[:, 64 * h : 64 * (h + 1)], in_=src[:, 64 * h : 64 * (h + 1)])
-            for h in range(2):
-                cols = slice(h * BANK // 2, (h + 1) * BANK // 2)
-                quantize(th_codes[c][:, cols], th_planes[c][:, cols], grouped[:, h * 2 * BANK : (h + 1) * 2 * BANK])
-
-        def intensities(i, t):
+        def a_slot(i, t):
             if t == 0:
                 a_banks[i] = take_bank()
             b, bank = a_banks[i]
@@ -253,97 +229,73 @@ def tile_noisy_or_symptom_prediction_s12_kernel(tc, x, w, u_words, u_scales, v_w
                     start=(g == 0),
                     stop=(g == PASSES - 1),
                 )
-            if t == PACK - 1:
-                grouped = staged("a_grouped", [P, PACK * P], BF16, 2)
-                dst = grouped[:].rearrange("p (m t) -> p m t", t=PACK)
-                src = bank[:].rearrange("p (t m) -> p m t", t=PACK)
-                if i < ACT_A_UNTIL:
+            if t == SLOTS - 1:
+                grouped = staged("a_grouped", [P, SLOTS * P], BF16, 2)
+                dst = grouped[:].rearrange("p (m t) -> p m t", t=SLOTS)
+                src = bank[:].rearrange("p (t m) -> p m t", t=SLOTS)
+                if i < FIRST_Z_ROUND:
                     nc.scalar.activation(out=dst, in_=src, func=ACT.Relu)
                 else:
                     nc.vector.tensor_scalar(out=dst, in0=src, scalar1=0.0, scalar2=None, op0=ALU.max)
                 free_banks.append(b)
-                later(DELAY_QA, lambda: quantize(a_codes[i][:], a_planes[i][:], grouped[:]))
+                later(DELAY, lambda: quantize(a_codes[i][:], a_planes[i][:], grouped[:]))
             step_done()
 
-        def symptoms(n):
+        def z_chunk(n):
             i, c = divmod(n, CHUNKS)
-            pair = n // 2
-            if c % 2 == 0:
-                e_tiles[pair] = staged("e", [P, 2 * BANK], F32, 6)
+            if c == 0:
+                e_tiles[i] = staged("e", [P, S], F32, 4)
             b, bank = take_bank()
             nc.tensor.matmul_mx(
                 out=bank[:],
                 lhsT=a_codes[i][:].bitcast(FP8X4),
                 lhsT_scale=a_planes[i][:],
-                rhs=th_codes[c][:].bitcast(FP8X4),
-                rhs_scale=th_planes[c][:],
+                rhs=theta_codes[c][:].bitcast(FP8X4),
+                rhs_scale=theta_planes[c][:],
                 start=True,
                 stop=True,
             )
-            cols = slice((c % 2) * BANK, (c % 2 + 1) * BANK)
-            nc.scalar.activation(out=e_tiles[pair][:, cols], in_=bank[:], func=ACT.Exp, scale=-1.0)
+            nc.scalar.activation(out=e_tiles[i][:, c * BANK : (c + 1) * BANK], in_=bank[:], func=ACT.Exp, scale=-1.0)
             free_banks.append(b)
-            if n >= FINE_FROM:
-                later(DELAY_FIN, lambda: finish(pair, c % 2, c % 2 + 1))
-            elif c % 2 == 1:
-                later(DELAY_FIN, lambda: finish(pair, 0, 2))
+            width = 1 if i == TILES - 1 else 2
+            if (c + 1) % width == 0:
+                later(DELAY, lambda: finish(i, slice((c + 1 - width) * BANK, (c + 1) * BANK)))
             step_done()
 
-        def finish(pair, first, last):
-            i, half = divmod(pair, 2)
-            e = e_tiles[pair][:, first * BANK : last * BANK]
+        def finish(i, cols):
+            e = e_tiles[i][:, cols]
             nc.vector.tensor_scalar(out=e, in0=e, scalar1=-1.0, scalar2=1.0, op0=ALU.mult, op1=ALU.add)
-            nc.sync.dma_start(out=out[i * P : (i + 1) * P, (2 * half + first) * BANK : (2 * half + last) * BANK], in_=e)
+            nc.sync.dma_start(out=out[i * P : (i + 1) * P, cols], in_=e)
 
+        sort_u()
+        for g in range(PASSES):
+            prepare_w(g)
+        theta_chunk(0)
+        for i in range(LEAD):
+            theta_chunk(i + 1)
+            transpose_x(i, True)
 
-        for name in HEAD.split():
-            if name[0] == "x":
-                for half in range(2):
-                    transpose_x(int(name[1]), half)
-            elif name[0] == "w":
-                prepare_w(int(name[1]))
-            elif name[0] == "u":
-                sort_u()
-            elif name[0] == "p":
-                prepare_theta(int(name[1]))
-            elif name[0] == "s":
-                sort_x(int(name[1]))
-            else:
-                for t in range(PACK):
-                    theta_rows(int(name[1]), t)
-
-        rounds = TILES // GROUP
         woven = TILES * CHUNKS - TAIL_CHUNKS
-        theta_left = [(c, t) for c in range(HEAD_THETA, CHUNKS) for t in range(PACK)]
         done = 0
-        for r in range(rounds):
-            if r + LEAD < rounds:
-                for i in range(GROUP * (r + LEAD), GROUP * (r + LEAD + 1)):
-                    for half in range(2):
-                        transpose_x(i, half)
-            due = max(0, woven * (r + 1 - FIRST_Z_ROUND) // (rounds - FIRST_Z_ROUND))
-            count = due - done
-            slots = GROUP * PACK
-            for k in range(slots):
-                if k % PACK == SORT_AHEAD % PACK:
-                    sort_x(GROUP * (r + LEAD + 1 + SORT_ROUNDS) + k // PACK)
-                if r >= rounds - A_FIRST_ROUNDS:
-                    lo, hi = (0, 0)
-                elif Z_FIRST:
-                    lo, hi = -(-count * k // slots), -(-count * (k + 1) // slots)
-                else:
-                    lo, hi = count * k // slots, count * (k + 1) // slots
-                for n in range(done + lo, done + hi):
-                    symptoms(n)
-                for j in range(THETA_PER_ROUND * PACK * (k + 1) // slots - THETA_PER_ROUND * PACK * k // slots):
-                    if theta_left:
-                        theta_rows(*theta_left.pop(0))
-                intensities(GROUP * r + k // PACK, k % PACK)
-            if r >= rounds - A_FIRST_ROUNDS:
-                for n in range(done, due):
-                    symptoms(n)
+        for r in range(TILES):
+            ahead = r + LEAD
+            if ahead < PAIRS_FROM:
+                transpose_x(ahead, r < FIRST_Z_ROUND)
+            elif ahead < TILES and (ahead - PAIRS_FROM) % 2 == 0:
+                transpose_x(ahead, r < FIRST_Z_ROUND)
+                transpose_x(ahead + 1, r < FIRST_Z_ROUND)
+            if SORT_FROM <= ahead + 2 < TILES:
+                sort_x(ahead + 2)
+            due = max(0, woven * (r + 1 - FIRST_Z_ROUND) // (TILES - FIRST_Z_ROUND))
+            for t in range(SLOTS):
+                first, last = (math.ceil((due - done) * k / SLOTS) for k in (t, t + 1))
+                for n in range(done + first, done + last):
+                    z_chunk(n)
+                if r == 0:
+                    theta_slot(CHUNKS - 1, t)
+                a_slot(r, t)
             done = due
         for n in range(done, TILES * CHUNKS):
-            symptoms(n)
+            z_chunk(n)
         while pending:
             step_done()

@@ -183,8 +183,8 @@ def tile_noisy_or_symptom_prediction_s12_kernel(tc, x, w, u_words, u_scales, v_w
         def sort_x(i):
             x_sorted[i] = staged("x_sorted", [P, F // 2], F32, 4)
             nc.vector.tensor_copy(
-                out=x_sorted[i][:].rearrange("p (g u k) -> p g u k", g=PASSES, u=2),
-                in_=x_raw[i][:].bitcast(F32).rearrange("p (g k u) -> p g u k", g=PASSES, u=2),
+                out=x_sorted[i][:].rearrange("p (g u k n) -> p g k u n", g=PASSES, u=2, n=4),
+                in_=x_raw[i][:].bitcast(F32).rearrange("p (g k n u) -> p g k u n", g=PASSES, u=2, n=4),
             )
 
         def transpose_x(i, on_scalar_only):
@@ -198,9 +198,9 @@ def tile_noisy_or_symptom_prediction_s12_kernel(tc, x, w, u_words, u_scales, v_w
                     else:
                         words = x_raw[i][:].bitcast(F32)[:, PASS_WORDS * g + u : PASS_WORDS * (g + 1) : 2]
                     nc.tensor.transpose(bank[:, n * P : (n + 1) * P], words, ident[:])
-                src = bank[:].rearrange("p (g u m) -> p g m u", g=2, u=2)
+                src = bank[:].rearrange("p (g u m n) -> p g m u n", g=2, u=2, n=2)
                 dst = x_grouped[i][:].bitcast(F32)[:, half * BANK : (half + 1) * BANK]
-                dst = dst.rearrange("p (g m u) -> p g m u", g=2, u=2)
+                dst = dst.rearrange("p (g m n u) -> p g m u n", g=2, u=2, n=2)
                 if on_scalar_only or (2 * i + half + 1) % VECTOR_BANK_EVERY != 0:
                     nc.scalar.copy(out=dst, in_=src)
                 else:
@@ -231,8 +231,8 @@ def tile_noisy_or_symptom_prediction_s12_kernel(tc, x, w, u_words, u_scales, v_w
                 )
             if t == SLOTS - 1:
                 grouped = staged("a_grouped", [P, SLOTS * P], BF16, 2)
-                dst = grouped[:].rearrange("p (m t) -> p m t", t=SLOTS)
-                src = bank[:].rearrange("p (t m) -> p m t", t=SLOTS)
+                dst = grouped[:].rearrange("p (m n t) -> p m t n", t=SLOTS, n=2)
+                src = bank[:].rearrange("p (t m n) -> p m t n", t=SLOTS, n=2)
                 if i < FIRST_Z_ROUND:
                     nc.scalar.activation(out=dst, in_=src, func=ACT.Relu)
                 else:

@@ -35,6 +35,13 @@ SORT_FROM = 5
 VECTOR_BANK_EVERY = 4
 DELAY = 3
 
+STAGING_BUFS = 2
+X_BUFS = 4
+X_CODE_BUFS = 6
+RESULT_BUFS = 4
+
+assert LEAD + 2 == CHUNKS
+
 
 def tile_noisy_or_symptom_prediction_s12_kernel(tc, x, w, u_words, u_scales, v_words, v_scales, out):
     nc = tc.nc
@@ -65,21 +72,19 @@ def tile_noisy_or_symptom_prediction_s12_kernel(tc, x, w, u_words, u_scales, v_w
         a_codes = [kept("a_codes%d" % i, [P, P], U32) for i in range(TILES)]
         a_planes = [kept("a_plane%d" % i, [P, P], U8) for i in range(TILES)]
         ident = kept("ident", [P, P], F32)
-        warm = kept("warm", [P, 16], F32)
 
         nc.vector.memset(u_raw_plane[:].bitcast(I32), 0)
         nc.vector.memset(v_plane[:].bitcast(I32), 0)
         make_identity(nc, ident[:])
-        nc.scalar.activation(out=warm[:, 0:1], in_=ident[:, 0:1], func=ACT.Exp)
 
         def load_bytes(tile, words):
             nc.sync.dma_start(out=tile[:].bitcast(I32), in_=words[0].bitcast(I32))
 
         def load_plane(plane, scales):
-            for n in range(4):
+            for quadrant in range(4):
                 nc.sync.dma_start(
-                    out=plane[32 * n : 32 * n + 4, :].bitcast(I32),
-                    in_=scales[0, 4 * n : 4 * n + 4, :].bitcast(I32),
+                    out=plane[32 * quadrant : 32 * quadrant + 4, :].bitcast(I32),
+                    in_=scales[0, 4 * quadrant : 4 * quadrant + 4, :].bitcast(I32),
                 )
 
         def load_w(g):
@@ -123,15 +128,15 @@ def tile_noisy_or_symptom_prediction_s12_kernel(tc, x, w, u_words, u_scales, v_w
             nc.vector.quantize_mx(out=codes.bitcast(FP8X4), scales=plane, in_=grouped)
 
         def quantize_halves(codes, plane, grouped):
-            half = codes.shape[1] // 2
-            for h in range(2):
-                cols = slice(h * half, (h + 1) * half)
-                quantize(codes[:, cols], plane[:, cols], grouped[:, SLOTS * h * half : SLOTS * (h + 1) * half])
+            width = codes.shape[1] // 2
+            for half in range(2):
+                cols = slice(half * width, (half + 1) * width)
+                quantize(codes[:, cols], plane[:, cols], grouped[:, SLOTS * cols.start : SLOTS * cols.stop])
 
         def sort_u():
             nc.vector.tensor_copy(
-                out=u_codes[:].bitcast(I32).rearrange("p (t Q h) -> p t Q h", t=SLOTS, h=2),
-                in_=u_raw[:].bitcast(I32).rearrange("p (Q t h) -> p t Q h", t=SLOTS, h=2),
+                out=u_codes[:].bitcast(I32).rearrange("p (t Q y) -> p t Q y", t=SLOTS, y=2),
+                in_=u_raw[:].bitcast(I32).rearrange("p (Q t y) -> p t Q y", t=SLOTS, y=2),
             )
             nc.vector.tensor_copy(
                 out=u_plane[:].bitcast(I32).rearrange("p (t Q) -> p t Q", t=SLOTS),
@@ -139,11 +144,12 @@ def tile_noisy_or_symptom_prediction_s12_kernel(tc, x, w, u_words, u_scales, v_w
             )
 
         def prepare_w(g):
-            grouped = staged("w_grouped", [P, SLOTS * D], BF16, 2)
-            src = w_raw[g][:].rearrange("p (j Q t i) -> p Q t j i", j=SLOTS, t=SLOTS, i=4)
-            dst = grouped[:].rearrange("p (t Q i j) -> p Q t j i", t=SLOTS, i=4, j=SLOTS)
-            for h in range(2):
-                nc.vector.tensor_copy(out=dst[:, :, 2 * h : 2 * h + 2], in_=src[:, :, 2 * h : 2 * h + 2])
+            grouped = staged("w_grouped", [P, SLOTS * D], BF16, STAGING_BUFS)
+            src = w_raw[g][:].rearrange("p (j Q t a) -> p Q t j a", j=SLOTS, t=SLOTS, a=4)
+            dst = grouped[:].rearrange("p (t Q a j) -> p Q t j a", t=SLOTS, a=4, j=SLOTS)
+            for half in range(2):
+                slots = slice(2 * half, 2 * half + 2)
+                nc.vector.tensor_copy(out=dst[:, :, slots], in_=src[:, :, slots])
             quantize_halves(w_codes[g], w_planes[g], grouped)
 
         theta_rows, x_sorted, x_grouped, x_codes, x_planes, a_banks, e_tiles = {}, {}, {}, {}, {}, {}, {}
@@ -172,35 +178,36 @@ def tile_noisy_or_symptom_prediction_s12_kernel(tc, x, w, u_words, u_scales, v_w
                 theta_slot(c, t)
 
         def prepare_theta(c):
-            grouped = staged("theta_grouped", [P, SLOTS * BANK], BF16, 2)
-            src = theta_rows[c][:].rearrange("p (t s i) -> p s t i", t=SLOTS, i=4)
-            dst = grouped[:].rearrange("p (s i t) -> p s t i", t=SLOTS, i=4)
-            half = BANK // 4 // 2
-            for h in range(2):
-                nc.vector.tensor_copy(out=dst[:, half * h : half * (h + 1)], in_=src[:, half * h : half * (h + 1)])
+            grouped = staged("theta_grouped", [P, SLOTS * BANK], BF16, STAGING_BUFS)
+            src = theta_rows[c][:].rearrange("p (t s n) -> p s t n", t=SLOTS, n=4)
+            dst = grouped[:].rearrange("p (s n t) -> p s t n", t=SLOTS, n=4)
+            runs = src.shape[1] // 2
+            for half in range(2):
+                part = slice(half * runs, (half + 1) * runs)
+                nc.vector.tensor_copy(out=dst[:, part], in_=src[:, part])
             quantize_halves(theta_codes[c], theta_planes[c], grouped)
 
         def sort_x(i):
-            x_sorted[i] = staged("x_sorted", [P, F // 2], F32, 4)
+            x_sorted[i] = staged("x_sorted", [P, F // 2], F32, X_BUFS)
             nc.vector.tensor_copy(
-                out=x_sorted[i][:].rearrange("p (g u k n) -> p g k u n", g=PASSES, u=2, n=4),
-                in_=x_raw[i][:].bitcast(F32).rearrange("p (g k n u) -> p g k u n", g=PASSES, u=2, n=4),
+                out=x_sorted[i][:].rearrange("p (g o k n) -> p g k o n", g=PASSES, o=2, n=4),
+                in_=x_raw[i][:].bitcast(F32).rearrange("p (g k n o) -> p g k o n", g=PASSES, o=2, n=4),
             )
 
         def transpose_x(i, on_scalar_only):
-            x_grouped[i] = staged("x_grouped", [P, F], BF16, 4)
+            x_grouped[i] = staged("x_grouped", [P, F], BF16, X_BUFS)
             for half in range(2):
                 b, bank = take_bank()
-                for n in range(4):
-                    g, u = 2 * half + n // 2, n % 2
+                for quarter in range(4):
+                    g, o = 2 * half + quarter // 2, quarter % 2
                     if i in x_sorted:
-                        words = x_sorted[i][:, PASS_WORDS * g + P * u : PASS_WORDS * g + P * (u + 1)]
+                        words = x_sorted[i][:, PASS_WORDS * g + P * o : PASS_WORDS * g + P * (o + 1)]
                     else:
-                        words = x_raw[i][:].bitcast(F32)[:, PASS_WORDS * g + u : PASS_WORDS * (g + 1) : 2]
-                    nc.tensor.transpose(bank[:, n * P : (n + 1) * P], words, ident[:])
-                src = bank[:].rearrange("p (g u m n) -> p g m u n", g=2, u=2, n=2)
+                        words = x_raw[i][:].bitcast(F32)[:, PASS_WORDS * g + o : PASS_WORDS * (g + 1) : 2]
+                    nc.tensor.transpose(bank[:, quarter * P : (quarter + 1) * P], words, ident[:])
+                src = bank[:].rearrange("p (g o m n) -> p g m o n", g=2, o=2, n=2)
                 dst = x_grouped[i][:].bitcast(F32)[:, half * BANK : (half + 1) * BANK]
-                dst = dst.rearrange("p (g m n u) -> p g m u n", g=2, u=2, n=2)
+                dst = dst.rearrange("p (g m n o) -> p g m o n", g=2, o=2, n=2)
                 if on_scalar_only or (2 * i + half + 1) % VECTOR_BANK_EVERY != 0:
                     nc.scalar.copy(out=dst, in_=src)
                 else:
@@ -211,8 +218,8 @@ def tile_noisy_or_symptom_prediction_s12_kernel(tc, x, w, u_words, u_scales, v_w
                 step_done()
 
         def quantize_x(i):
-            x_codes[i] = staged("x_codes", [P, PASSES * P], U32, 6)
-            x_planes[i] = staged("x_plane", [P, PASSES * P], U8, 6)
+            x_codes[i] = staged("x_codes", [P, PASSES * P], U32, X_CODE_BUFS)
+            x_planes[i] = staged("x_plane", [P, PASSES * P], U8, X_CODE_BUFS)
             quantize(x_codes[i][:], x_planes[i][:], x_grouped[i][:])
 
         def a_slot(i, t):
@@ -230,7 +237,7 @@ def tile_noisy_or_symptom_prediction_s12_kernel(tc, x, w, u_words, u_scales, v_w
                     stop=(g == PASSES - 1),
                 )
             if t == SLOTS - 1:
-                grouped = staged("a_grouped", [P, SLOTS * P], BF16, 2)
+                grouped = staged("a_grouped", [P, SLOTS * P], BF16, STAGING_BUFS)
                 dst = grouped[:].rearrange("p (m n t) -> p m t n", t=SLOTS, n=2)
                 src = bank[:].rearrange("p (t m n) -> p m t n", t=SLOTS, n=2)
                 if i < FIRST_Z_ROUND:
@@ -241,10 +248,10 @@ def tile_noisy_or_symptom_prediction_s12_kernel(tc, x, w, u_words, u_scales, v_w
                 later(DELAY, lambda: quantize(a_codes[i][:], a_planes[i][:], grouped[:]))
             step_done()
 
-        def z_chunk(n):
-            i, c = divmod(n, CHUNKS)
+        def z_chunk(z):
+            i, c = divmod(z, CHUNKS)
             if c == 0:
-                e_tiles[i] = staged("e", [P, S], F32, 4)
+                e_tiles[i] = staged("e", [P, S], F32, RESULT_BUFS)
             b, bank = take_bank()
             nc.tensor.matmul_mx(
                 out=bank[:],
@@ -257,9 +264,9 @@ def tile_noisy_or_symptom_prediction_s12_kernel(tc, x, w, u_words, u_scales, v_w
             )
             nc.scalar.activation(out=e_tiles[i][:, c * BANK : (c + 1) * BANK], in_=bank[:], func=ACT.Exp, scale=-1.0)
             free_banks.append(b)
-            width = 1 if i == TILES - 1 else 2
-            if (c + 1) % width == 0:
-                later(DELAY, lambda: finish(i, slice((c + 1 - width) * BANK, (c + 1) * BANK)))
+            together = 1 if i == TILES - 1 else 2
+            if (c + 1) % together == 0:
+                later(DELAY, lambda: finish(i, slice((c + 1 - together) * BANK, (c + 1) * BANK)))
             step_done()
 
         def finish(i, cols):
@@ -288,14 +295,15 @@ def tile_noisy_or_symptom_prediction_s12_kernel(tc, x, w, u_words, u_scales, v_w
                 sort_x(ahead + 2)
             due = max(0, woven * (r + 1 - FIRST_Z_ROUND) // (TILES - FIRST_Z_ROUND))
             for t in range(SLOTS):
-                first, last = (math.ceil((due - done) * k / SLOTS) for k in (t, t + 1))
-                for n in range(done + first, done + last):
-                    z_chunk(n)
+                first = done + math.ceil((due - done) * t / SLOTS)
+                last = done + math.ceil((due - done) * (t + 1) / SLOTS)
+                for z in range(first, last):
+                    z_chunk(z)
                 if r == 0:
                     theta_slot(CHUNKS - 1, t)
                 a_slot(r, t)
             done = due
-        for n in range(done, TILES * CHUNKS):
-            z_chunk(n)
+        for z in range(done, TILES * CHUNKS):
+            z_chunk(z)
         while pending:
             step_done()

import math
from contextlib import ExitStack

import concourse.mybir as mybir
from concourse.masks import make_identity

M, F, D, R, S = 2048, 2048, 512, 512, 2048
FLOPS = 2 * M * F * D + 2 * D * R * S + 2 * M * D * S

F32 = mybir.dt.float32
BF16 = mybir.dt.bfloat16
I32 = mybir.dt.int32
U32 = mybir.dt.uint32
U8 = mybir.dt.uint8
FP8X4 = mybir.dt.float8_e4m3fn_x4
FP4X4 = mybir.dt.float4_e2m1fn_x4
ACT = mybir.ActivationFunctionType
ALU = mybir.AluOpType

P = 128
SLOTS = 4
K_PASS = P * SLOTS
BANK = 512
BANKS = 8
TILES = M // P
PASSES = F // K_PASS
CHUNKS = S // BANK
PASS_WORDS = K_PASS // 2

LEAD = 2
FIRST_Z_ROUND = 3
TAIL_CHUNKS = 6
PAIRS_FROM = 4
SORT_FROM = 5
VECTOR_BANK_EVERY = 4
DELAY = 3

STAGING_BUFS = 2
X_BUFS = 4
X_CODE_BUFS = 6
RESULT_BUFS = 4

assert LEAD + 2 == CHUNKS


def tile_noisy_or_symptom_prediction_s12_kernel(tc, x, w, u_words, u_scales, v_words, v_scales, out):
    nc = tc.nc
    with ExitStack() as ctx:
        keep = ctx.enter_context(tc.tile_pool(name="keep", bufs=1))
        stage = ctx.enter_context(tc.tile_pool(name="stage", bufs=1))
        psum = ctx.enter_context(tc.psum_pool(name="psum", bufs=1))
        ctx.enter_context(tc.manual_schedule())

        def kept(name, shape, dtype):
            return keep.tile(shape, dtype, name=name, align_bytes=64)

        def staged(name, shape, dtype, bufs):
            return stage.tile(shape, dtype, name=name, tag=name, bufs=bufs, align_bytes=64)

        w_raw = [kept("w_raw%d" % g, [P, SLOTS * D], BF16) for g in range(PASSES)]
        x_raw = [kept("x_raw%d" % i, [P, F], BF16) for i in range(TILES)]
        u_raw = kept("u_raw", [P, 2 * D], U8)
        u_raw_plane = kept("u_raw_plane", [P, D], U8)
        u_codes = kept("u_codes", [P, 2 * D], U8)
        u_plane = kept("u_plane", [P, D], U8)
        v_codes = kept("v_codes", [P, 2 * S], U8)
        v_plane = kept("v_plane", [P, S], U8)
        w_codes = [kept("w_codes%d" % g, [P, D], U32) for g in range(PASSES)]
        w_planes = [kept("w_plane%d" % g, [P, D], U8) for g in range(PASSES)]
        theta_codes = [kept("theta_codes%d" % c, [P, BANK], U32) for c in range(CHUNKS)]
        theta_planes = [kept("theta_plane%d" % c, [P, BANK], U8) for c in range(CHUNKS)]
        a_codes = [kept("a_codes%d" % i, [P, P], U32) for i in range(TILES)]
        a_planes = [kept("a_plane%d" % i, [P, P], U8) for i in range(TILES)]
        ident = kept("ident", [P, P], F32)

        nc.vector.memset(u_raw_plane[:].bitcast(I32), 0)
        nc.vector.memset(v_plane[:].bitcast(I32), 0)
        make_identity(nc, ident[:])

        def load_bytes(tile, words):
            nc.sync.dma_start(out=tile[:].bitcast(I32), in_=words[0].bitcast(I32))

        def load_plane(plane, scales):
            for quadrant in range(4):
                nc.sync.dma_start(
                    out=plane[32 * quadrant : 32 * quadrant + 4, :].bitcast(I32),
                    in_=scales[0, 4 * quadrant : 4 * quadrant + 4, :].bitcast(I32),
                )

        def load_w(g):
            rows = w[g * K_PASS : (g + 1) * K_PASS, :]
            nc.sync.dma_start(out=w_raw[g][:], in_=rows.rearrange("(p j) d -> p (j d)", j=SLOTS))

        def load_x(i):
            nc.sync.dma_start(out=x_raw[i][:], in_=x[i * P : (i + 1) * P, :])

        load_bytes(u_raw, u_words)
        load_plane(u_raw_plane, u_scales)
        load_w(0)
        load_bytes(v_codes, v_words)
        load_plane(v_plane, v_scales)
        load_w(1)
        load_x(0)
        load_w(2)
        load_w(3)
        for i in range(1, TILES):
            load_x(i)

        free_banks = list(range(BANKS))

        def take_bank():
            b = free_banks.pop(0)
            return b, psum.tile([P, BANK], F32, name="bank%d" % b, tag="bank%d" % b)

        pending = []

        def later(steps, work):
            pending.append([steps, work])

        def step_done():
            for entry in list(pending):
                entry[0] = entry[0] - 1
                if entry[0] == 0:
                    pending.remove(entry)
                    entry[1]()

        def quantize(codes, plane, grouped):
            nc.vector.quantize_mx(out=codes.bitcast(FP8X4), scales=plane, in_=grouped)

        def quantize_halves(codes, plane, grouped):
            width = codes.shape[1] // 2
            for half in range(2):
                cols = slice(half * width, (half + 1) * width)
                quantize(codes[:, cols], plane[:, cols], grouped[:, SLOTS * cols.start : SLOTS * cols.stop])

        def sort_u():
            nc.vector.tensor_copy(
                out=u_codes[:].bitcast(I32).rearrange("p (t Q y) -> p t Q y", t=SLOTS, y=2),
                in_=u_raw[:].bitcast(I32).rearrange("p (Q t y) -> p t Q y", t=SLOTS, y=2),
            )
            nc.vector.tensor_copy(
                out=u_plane[:].bitcast(I32).rearrange("p (t Q) -> p t Q", t=SLOTS),
                in_=u_raw_plane[:].bitcast(I32).rearrange("p (Q t) -> p t Q", t=SLOTS),
            )

        def prepare_w(g):
            grouped = staged("w_grouped", [P, SLOTS * D], BF16, STAGING_BUFS)
            src = w_raw[g][:].rearrange("p (j Q t a) -> p Q t j a", j=SLOTS, t=SLOTS, a=4)
            dst = grouped[:].rearrange("p (t Q a j) -> p Q t j a", t=SLOTS, a=4, j=SLOTS)
            for half in range(2):
                slots = slice(2 * half, 2 * half + 2)
                nc.vector.tensor_copy(out=dst[:, :, slots], in_=src[:, :, slots])
            quantize_halves(w_codes[g], w_planes[g], grouped)

        theta_rows, x_sorted, x_grouped, x_codes, x_planes, a_banks, e_tiles = {}, {}, {}, {}, {}, {}, {}

        def theta_slot(c, t):
            if t == 0:
                theta_rows[c] = staged("theta_rows", [P, SLOTS * BANK], BF16, CHUNKS)
            b, bank = take_bank()
            nc.tensor.matmul_mx(
                out=bank[:],
                lhsT=u_codes[:, 2 * P * t : 2 * P * (t + 1)].bitcast(FP4X4),
                lhsT_scale=u_plane[:, P * t : P * (t + 1)],
                rhs=v_codes[:, 2 * BANK * c : 2 * BANK * (c + 1)].bitcast(FP4X4),
                rhs_scale=v_plane[:, BANK * c : BANK * (c + 1)],
                start=True,
                stop=True,
            )
            nc.scalar.copy(out=theta_rows[c][:, BANK * t : BANK * (t + 1)], in_=bank[:])
            free_banks.append(b)
            if t == SLOTS - 1:
                later(2 * DELAY, lambda: prepare_theta(c))
            step_done()

        def theta_chunk(c):
            for t in range(SLOTS):
                theta_slot(c, t)

        def prepare_theta(c):
            grouped = staged("theta_grouped", [P, SLOTS * BANK], BF16, STAGING_BUFS)
            src = theta_rows[c][:].rearrange("p (t s n) -> p s t n", t=SLOTS, n=4)
            dst = grouped[:].rearrange("p (s n t) -> p s t n", t=SLOTS, n=4)
            runs = src.shape[1] // 2
            for half in range(2):
                part = slice(half * runs, (half + 1) * runs)
                nc.vector.tensor_copy(out=dst[:, part], in_=src[:, part])
            quantize_halves(theta_codes[c], theta_planes[c], grouped)

        def sort_x(i):
            x_sorted[i] = staged("x_sorted", [P, F // 2], F32, X_BUFS)
            nc.vector.tensor_copy(
                out=x_sorted[i][:].rearrange("p (g o k n) -> p g k o n", g=PASSES, o=2, n=4),
                in_=x_raw[i][:].bitcast(F32).rearrange("p (g k n o) -> p g k o n", g=PASSES, o=2, n=4),
            )

        def transpose_x(i, on_scalar_only):
            x_grouped[i] = staged("x_grouped", [P, F], BF16, X_BUFS)
            for half in range(2):
                b, bank = take_bank()
                for quarter in range(4):
                    g, o = 2 * half + quarter // 2, quarter % 2
                    if i in x_sorted:
                        words = x_sorted[i][:, PASS_WORDS * g + P * o : PASS_WORDS * g + P * (o + 1)]
                    else:
                        words = x_raw[i][:].bitcast(F32)[:, PASS_WORDS * g + o : PASS_WORDS * (g + 1) : 2]
                    nc.tensor.transpose(bank[:, quarter * P : (quarter + 1) * P], words, ident[:])
                src = bank[:].rearrange("p (g o m n) -> p g m o n", g=2, o=2, n=2)
                dst = x_grouped[i][:].bitcast(F32)[:, half * BANK : (half + 1) * BANK]
                dst = dst.rearrange("p (g m n o) -> p g m o n", g=2, o=2, n=2)
                if on_scalar_only or (2 * i + half + 1) % VECTOR_BANK_EVERY != 0:
                    nc.scalar.copy(out=dst, in_=src)
                else:
                    nc.vector.tensor_copy(out=dst, in_=src)
                free_banks.append(b)
                if half == 1:
                    later(DELAY, lambda: quantize_x(i))
                step_done()

        def quantize_x(i):
            x_codes[i] = staged("x_codes", [P, PASSES * P], U32, X_CODE_BUFS)
            x_planes[i] = staged("x_plane", [P, PASSES * P], U8, X_CODE_BUFS)
            quantize(x_codes[i][:], x_planes[i][:], x_grouped[i][:])

        def a_slot(i, t):
            if t == 0:
                a_banks[i] = take_bank()
            b, bank = a_banks[i]
            for g in range(PASSES):
                nc.tensor.matmul_mx(
                    out=bank[:, P * t : P * (t + 1)],
                    lhsT=w_codes[g][:, P * t : P * (t + 1)].bitcast(FP8X4),
                    lhsT_scale=w_planes[g][:, P * t : P * (t + 1)],
                    rhs=x_codes[i][:, P * g : P * (g + 1)].bitcast(FP8X4),
                    rhs_scale=x_planes[i][:, P * g : P * (g + 1)],
                    start=(g == 0),
                    stop=(g == PASSES - 1),
                )
            if t == SLOTS - 1:
                grouped = staged("a_grouped", [P, SLOTS * P], BF16, STAGING_BUFS)
                dst = grouped[:].rearrange("p (m n t) -> p m t n", t=SLOTS, n=2)
                src = bank[:].rearrange("p (t m n) -> p m t n", t=SLOTS, n=2)
                if i < FIRST_Z_ROUND:
                    nc.scalar.activation(out=dst, in_=src, func=ACT.Relu)
                else:
                    nc.vector.tensor_scalar(out=dst, in0=src, scalar1=0.0, scalar2=None, op0=ALU.max)
                free_banks.append(b)
                later(DELAY, lambda: quantize(a_codes[i][:], a_planes[i][:], grouped[:]))
            step_done()

        def z_chunk(z):
            i, c = divmod(z, CHUNKS)
            if c == 0:
                e_tiles[i] = staged("e", [P, S], F32, RESULT_BUFS)
            b, bank = take_bank()
            nc.tensor.matmul_mx(
                out=bank[:],
                lhsT=a_codes[i][:].bitcast(FP8X4),
                lhsT_scale=a_planes[i][:],
                rhs=theta_codes[c][:].bitcast(FP8X4),
                rhs_scale=theta_planes[c][:],
                start=True,
                stop=True,
            )
            nc.scalar.activation(out=e_tiles[i][:, c * BANK : (c + 1) * BANK], in_=bank[:], func=ACT.Exp, scale=-1.0)
            free_banks.append(b)
            together = 1 if i == TILES - 1 else 2
            if (c + 1) % together == 0:
                later(DELAY, lambda: finish(i, slice((c + 1 - together) * BANK, (c + 1) * BANK)))
            step_done()

        def finish(i, cols):
            e = e_tiles[i][:, cols]
            nc.vector.tensor_scalar(out=e, in0=e, scalar1=-1.0, scalar2=1.0, op0=ALU.mult, op1=ALU.add)
            nc.sync.dma_start(out=out[i * P : (i + 1) * P, cols], in_=e)

        sort_u()
        for g in range(PASSES):
            prepare_w(g)
        theta_chunk(0)
        for i in range(LEAD):
            theta_chunk(i + 1)
            transpose_x(i, True)

        woven = TILES * CHUNKS - TAIL_CHUNKS
        done = 0
        for r in range(TILES):
            ahead = r + LEAD
            if ahead < PAIRS_FROM:
                transpose_x(ahead, r < FIRST_Z_ROUND)
            elif ahead < TILES and (ahead - PAIRS_FROM) % 2 == 0:
                transpose_x(ahead, r < FIRST_Z_ROUND)
                transpose_x(ahead + 1, r < FIRST_Z_ROUND)
            if SORT_FROM <= ahead + 2 < TILES:
                sort_x(ahead + 2)
            due = max(0, woven * (r + 1 - FIRST_Z_ROUND) // (TILES - FIRST_Z_ROUND))
            for t in range(SLOTS):
                first = done + math.ceil((due - done) * t / SLOTS)
                last = done + math.ceil((due - done) * (t + 1) / SLOTS)
                for z in range(first, last):
                    z_chunk(z)
                if r == 0:
                    theta_slot(CHUNKS - 1, t)
                a_slot(r, t)
            done = due
        for z in range(done, TILES * CHUNKS):
            z_chunk(z)
        while pending:
            step_done()
